import numpy as np
import ml_dtypes


def mxq(x, axis, fmt="e4m3"):
    dtype, down = {"e4m3": (ml_dtypes.float8_e4m3fn, 7), "e5m2": (ml_dtypes.float8_e5m2, 14)}[fmt]
    v = np.moveaxis(np.asarray(x, np.float32).astype(ml_dtypes.bfloat16).astype(np.float64), axis, -1)
    blocks = v.reshape(v.shape[:-1] + (-1, 32))
    amax = np.abs(blocks).max(-1, keepdims=True)
    byte = np.maximum(np.where(amax > 0, np.frexp(amax)[1] - 1 + 127, 0) - down, 1)
    scale = np.exp2(byte - 127.0)
    codes = (blocks / scale).astype(np.float32).astype(dtype).astype(np.float64)
    return np.moveaxis((codes * scale).reshape(v.shape), -1, axis)


WIDE = False


def mx_kscale(k):
    if not WIDE:
        return np.ones(k)
    levels = np.array([10, -10, 5, -5, 0])
    if k % 512:
        return np.exp2(np.random.permutation(np.resize(levels, k // 32))).repeat(32)
    a = np.empty((k // 512, 16))
    for p in range(k // 512):
        a[p, :8] = np.random.permutation(np.resize(levels, 8))
        for g in range(8):
            far = levels[np.abs(levels - a[p, g]) >= 10]
            a[p, g + 8] = far[np.random.randint(len(far))]
    return np.exp2(a.ravel()).repeat(32)


def f64(x):
    return np.asarray(x).astype(np.float64)


def striped(idx):
    return np.tile(idx.reshape(-1, 16).T, (8, 1)).astype(np.uint16)


def unstriped(offs):
    return offs[:16].T.reshape(-1).astype(np.int64)


def striped8(idx):
    return np.concatenate([x.reshape(-1, 16).T for x in idx]).astype(np.uint16)


def runs(offs, k):
    lists = np.stack([offs[16 * r : 16 * r + 16].T.reshape(-1) for r in range(8)]).astype(np.int64)
    return lists[np.arange(k) % 512 // 64]


def pack_weight(w):
    k, n = w.shape
    w = f64(np.asarray(w, np.float32).astype(ml_dtypes.bfloat16)).reshape(k // 32, 32, n)
    amax = np.abs(w).max(1)
    byte = np.clip(np.where(amax > 0, np.frexp(amax)[1] - 1 + 127 - 7, 1), 1, 254)
    scaled = (w * np.exp2(127.0 - byte)[:, None, :]).reshape(k, n).astype(np.float32)
    words = np.ascontiguousarray(scaled.reshape(k // 512, 128, 4, n).transpose(0, 1, 3, 2)).astype(ml_dtypes.float8_e4m3fn).view(np.uint8)
    return words, np.ascontiguousarray(byte.astype(np.uint8).reshape(k // 512, 16, n))


def unpack_weight(words, scales):
    g, p, n, _ = words.shape
    vals = np.ascontiguousarray(words).view(ml_dtypes.float8_e4m3fn).astype(np.float64) * np.repeat(np.exp2(scales.astype(np.float64) - 127.0), 8, axis=1)[..., None]
    return vals.transpose(0, 1, 3, 2).reshape(g * 512, n)


E2M1 = np.array([0.0, 0.5, 1.0, 1.5, 2.0, 3.0, 4.0, 6.0, -0.0, -0.5, -1.0, -1.5, -2.0, -3.0, -4.0, -6.0])


def pack_fp4(w):
    k, n = w.shape
    w = f64(np.asarray(w, np.float32).astype(ml_dtypes.bfloat16)).reshape(k // 32, 32, n)
    amax = np.abs(w).max(1)
    mant, ex = np.frexp(amax / 6.0)
    byte = np.clip(np.where(amax > 0, np.where(mant > 0.5, ex, ex - 1) + 127, 1), 1, 254)
    scaled = (w * np.exp2(127.0 - byte)[:, None, :]).reshape(k, n).astype(np.float32)
    c = np.ascontiguousarray(scaled.reshape(k // 512, 128, 4, n).transpose(0, 1, 3, 2)).astype(ml_dtypes.float4_e2m1fn).view(np.uint8) & 0xF
    words = (c[..., 0::2] | (c[..., 1::2] << 4)).reshape(k // 512, 128, 2 * n)
    return np.ascontiguousarray(words), np.ascontiguousarray(byte.astype(np.uint8).reshape(k // 512, 16, n))


def unpack_fp4(words, scales):
    g, _, n = scales.shape
    words = np.ascontiguousarray(words).reshape(g, 128, n, 2)
    nib = np.empty((g, 128, n, 4), np.uint8)
    nib[..., 0::2] = words & 0xF
    nib[..., 1::2] = words >> 4
    vals = E2M1[nib] * np.repeat(np.exp2(scales.astype(np.float64) - 127.0), 8, axis=1)[..., None]
    return vals.transpose(0, 1, 3, 2).reshape(g * 512, n)


K, T, S, H, W, G, U = 512, 2048, 256, 512, 128, 2048, 1024


def setup_inputs():
    n = np.random.standard_normal
    s = mx_kscale(K)[:, None]
    packed_xT = pack_weight(n((K, T)) * s)
    packed_w1 = pack_fp4(n((K, H)) / np.sqrt(K) / s)
    packed_dT = pack_weight(n((K, G)) / s)
    perm = np.random.permutation(S)
    return {
        "x_words": packed_xT[0],
        "x_scales": packed_xT[1],
        "w1_words": packed_w1[0],
        "w1_scales": packed_w1[1],
        "gs": (np.random.uniform(0.5, 1.5, (K, 1)) * s).astype(np.float32),
        "d_words": packed_dT[0],
        "d_scales": packed_dT[1],
        "mem": n((H, U)).astype(np.float32),
        "offs": striped8(np.random.randint(0, T, (8, S))),
        "n1": striped(perm[:W]),
        "n2": striped(perm[W:]),
        "ka": striped8(np.random.randint(0, G, (8, H))),
        "kb": striped8(np.random.randint(0, G, (8, H))),
        "n3": striped(np.random.permutation(U)[:S]),
    }


def reference(x_words, x_scales, w1_words, w1_scales, gs, d_words, d_scales, mem, offs, n1, n2, ka, kb, n3):
    d_ka = unpack_weight(d_words, d_scales)[np.arange(K)[:, None], runs(ka, K)]
    xq = unpack_weight(x_words, x_scales)[np.arange(K)[:, None], runs(offs, K)]
    y = unpack_fp4(w1_words, w1_scales).T @ xq
    pb = y[:, unstriped(n2)]
    pa = y[:, unstriped(n1)]
    rb = pb - (0.5 * pa)
    ra = np.sqrt((pa) ** 2 + (pb) ** 2 + 0.25)
    ds = np.zeros((H, S))
    ds[:, unstriped(n1)] = ra
    dt = ds.copy()
    dt[:, unstriped(n2)] = rb
    z = f64(gs) * dt
    zq = mxq(z, 0, "e4m3")
    d_kb = unpack_weight(d_words, d_scales)[np.arange(K)[:, None], runs(kb, K)]
    h = 0.0625 * (d_ka.T @ zq + d_kb.T @ zq)
    out = f64(mem).copy()
    out[:, unstriped(n3)] = h
    return out

@@ -1,0 +1,175 @@
+from contextlib import ExitStack
+
+import concourse.mybir as mybir
+
+K, T, S, H, W, G, U = 512, 2048, 256, 512, 128, 2048, 1024
+FLOPS = 2 * K * H * S * 3
+
+F32 = mybir.dt.float32
+BF16 = mybir.dt.bfloat16
+I32 = mybir.dt.int32
+U32 = mybir.dt.uint32
+U16 = mybir.dt.uint16
+U8 = mybir.dt.uint8
+FP8X4 = mybir.dt.float8_e4m3fn_x4
+FP4X4 = mybir.dt.float4_e2m1fn_x4
+ALU = mybir.AluOpType
+ACT = mybir.ActivationFunctionType
+
+P = 128
+PACK = 4
+QUAD = 32
+OCTET = 8
+HALF = S // 2
+PIECE = 256
+
+
+def tile_picked_hdaqpolarpage_none_p_kernel(
+    tc, x_words, x_scales, w1_words, w1_scales, gs, d_words, d_scales, mem, offs, n1, n2, ka, kb, n3, out
+):
+    nc = tc.nc
+    with ExitStack() as ctx:
+        lists = ctx.enter_context(tc.tile_pool(name="lists", bufs=1))
+        sb = ctx.enter_context(tc.tile_pool(name="sb", bufs=1))
+        psum = ctx.enter_context(tc.psum_pool(name="psum", bufs=8))
+
+        def load_list(src, name):
+            tile = lists.tile(list(src.shape), U16, name=name)
+            nc.sync.dma_start(tile[:], src)
+            return tile
+
+        def load_scale_table(queue, scales, name, tag):
+            table = sb.tile([P, scales.shape[2]], U8, name=name, tag=tag, align_bytes=64)
+            rows = scales[0].bitcast(I32)
+            queue.dma_start(table[:].bitcast(I32), rows.unsqueeze(1).to_broadcast([16, OCTET, rows.shape[1]]))
+            return table
+
+        def move_scale_rows(queue, plane, picked):
+            for i in range(1, 4):
+                queue.dma_start(plane[i:P:QUAD, :].bitcast(I32), picked[OCTET * i : P : QUAD, :].bitcast(I32))
+
+        offs_sb = load_list(offs, "offs_sb")
+        xw_table = sb.tile([P, T], I32, tag="word_table", align_bytes=64)
+        nc.scalar.dma_start(xw_table[:], x_words[0].rearrange("p n t -> p (n t)").bitcast(I32))
+        xs_table = load_scale_table(nc.sync, x_scales, "xs_table", "scale_table")
+        w1w_raw = sb.tile([P, 2 * H], U8, align_bytes=64)
+        nc.sync.dma_start(w1w_raw[:].bitcast(I32), w1_words[0].bitcast(I32))
+        w1s_raw = sb.tile([P, H], U8, align_bytes=64)
+        for q in range(4):
+            rows = w1_scales[0][4 * q : 4 * q + 4, :].bitcast(I32)
+            nc.sync.dma_start(w1s_raw[QUAD * q : QUAD * (q + 1), :].bitcast(I32), rows.partition_broadcast(OCTET))
+        n1_sb = load_list(n1, "n1_sb")
+        n2_sb = load_list(n2, "n2_sb")
+        ka_sb = load_list(ka, "ka_sb")
+        kb_sb = load_list(kb, "kb_sb")
+        n3_sb = load_list(n3, "n3_sb")
+        xs_plane = sb.tile([P, S], U8, align_bytes=64)
+        nc.vector.memset(xs_plane[:].bitcast(I32), 0)
+
+        xs_picked = sb.tile([P, S], U8, align_bytes=64)
+        nc.vector.tensor_copy(xs_picked[:], xs_table[:].indirect(offs_sb[:]))
+        move_scale_rows(nc.scalar, xs_plane, xs_picked)
+        for q in range(4):
+            row = slice(QUAD * q, QUAD * q + 1)
+            nc.vector.tensor_copy(xs_plane[row, :].bitcast(I32), xs_picked[row, :].bitcast(I32))
+        ds_table = load_scale_table(nc.sync, d_scales, "ds_table", "scale_table")
+
+        w1w = sb.tile([P, 2 * H], U8, align_bytes=64)
+        nc.scalar.copy(
+            w1w[:].bitcast(U16).rearrange("p (t m) -> p t m", t=PACK),
+            w1w_raw[:].bitcast(U16).rearrange("p (m t) -> p t m", t=PACK),
+        )
+        w1s = sb.tile([P, H], U8, align_bytes=64)
+        nc.vector.tensor_copy(
+            w1s[:].rearrange("p (t m) -> p t m", t=PACK), w1s_raw[:].rearrange("p (m t) -> p t m", t=PACK)
+        )
+        xw_picked = sb.tile([P, S], U32, tag="gs", align_bytes=64)
+        nc.vector.tensor_copy(xw_picked[:], xw_table[:].bitcast(U32).indirect(offs_sb[:]))
+
+        dw_table = sb.tile([P, G], I32, tag="word_table", align_bytes=64)
+        nc.sync.dma_start(dw_table[:], d_words[0].rearrange("p n t -> p (n t)").bitcast(I32))
+
+        y = []
+        for t in range(PACK):
+            acc = psum.tile([P, S], F32, tag="acc", name=f"y_acc{t}")
+            nc.tensor.matmul_mx(
+                out=acc[:],
+                lhsT=w1w[:, 2 * P * t : 2 * P * (t + 1)].bitcast(FP4X4),
+                lhsT_scale=w1s[:, P * t : P * (t + 1)],
+                rhs=xw_picked[:].bitcast(FP8X4),
+                rhs_scale=xs_plane[:],
+                start=True,
+                stop=True,
+            )
+            y.append(sb.tile([P, S], F32, tag=f"page{t}", name=f"y{t}", align_bytes=64))
+            nc.vector.tensor_copy(y[t][:], acc[:])
+
+        gs_sb = sb.tile([P, PACK], F32, tag="gs", align_bytes=64)
+        nc.sync.dma_start(gs_sb[:], gs.rearrange("(p t) o -> p (t o)", t=PACK))
+
+        rb = sb.tile([P, PACK, W], F32)
+        radicand = sb.tile([P, PACK, W], F32)
+        for t in range(PACK):
+            pair = sb.tile([P, 2 * W], F32, name=f"pair{t}")
+            pa, pb = pair[:, :W], pair[:, W:]
+            nc.scalar.activation(pa, y[t][:].indirect(n1_sb[:]), ACT.Copy)
+            nc.scalar.activation(pb, y[t][:].indirect(n2_sb[:]), ACT.Copy)
+            nc.vector.scalar_tensor_tensor(rb[:, t, :], pa, -0.5, pb, ALU.mult, ALU.add)
+            squares = sb.tile([P, 2 * W], F32, name=f"squares{t}")
+            nc.vector.tensor_tensor(squares[:], pair[:], pair[:], ALU.mult)
+            nc.vector.scalar_tensor_tensor(radicand[:, t, :], squares[:, :W], 0.25, squares[:, W:], ALU.add, ALU.add)
+
+        page = []
+        for m in range(H // P):
+            page.append(sb.tile([P, U], F32, tag=f"page{m}", name=f"page_sb{m}", align_bytes=64))
+            nc.sync.dma_start(page[m][:], mem[P * m : P * (m + 1), :])
+
+        dt = [sb.tile([P, S], F32, name=f"dt{t}") for t in range(PACK)]
+        for t in range(PACK):
+            nc.scalar.activation(dt[t][:].indirect(n2_sb[:]), rb[:, t, :], ACT.Copy)
+        ra = sb.tile([P, PACK, W], F32)
+        nc.scalar.activation(ra[:], radicand[:], ACT.Sqrt)
+
+        ds_picked = sb.tile([P, 2 * H], U8, align_bytes=64)
+        dw_picked = sb.tile([P, 2 * H], U32, align_bytes=64)
+        pieces = [(H * c + s0, codes[:, s0 // 16 : (s0 + PIECE) // 16]) for c, codes in enumerate((ka_sb, kb_sb)) for s0 in range(0, H, PIECE)]
+        for c0, offsets in pieces:
+            nc.vector.tensor_copy(ds_picked[:, c0 : c0 + PIECE], ds_table[:].indirect(offsets))
+        ds_plane = sb.tile([P, 2 * H], U8, align_bytes=64)
+        nc.vector.tensor_copy(ds_plane[:].bitcast(I32), ds_picked[:].bitcast(I32))
+        move_scale_rows(nc.sync, ds_plane, ds_picked)
+        for c0, offsets in pieces:
+            nc.vector.tensor_copy(dw_picked[:, c0 : c0 + PIECE], dw_table[:].bitcast(U32).indirect(offsets))
+
+        z = [sb.tile([P, HALF, PACK], BF16, name=f"z{half}", tag=tag, align_bytes=64) for half, tag in enumerate(("scale_table", "word_table"))]
+        for t in range(PACK):
+            nc.scalar.activation(dt[t][:].indirect(n1_sb[:]), ra[:, t, :], ACT.Copy)
+            for half in range(2):
+                nc.vector.tensor_scalar(
+                    z[half][:, :, t], dt[t][:, HALF * half : HALF * (half + 1)], gs_sb[:, t : t + 1], None, ALU.mult
+                )
+        zw = sb.tile([P, S], U32, align_bytes=64)
+        zs = sb.tile([P, S], U8, align_bytes=64)
+        for half in range(2):
+            cols = slice(HALF * half, HALF * (half + 1))
+            nc.vector.quantize_mx(out=zw[:, cols].bitcast(FP8X4), scales=zs[:, cols], in_=z[half][:].rearrange("p j t -> p (j t)"))
+
+        steps = [(0, 0, HALF), (1, 0, HALF), (0, HALF, S), (1, HALF, S), (2, 0, S), (3, 0, S)]
+        for m, j0, j1 in steps:
+            acc = psum.tile([P, j1 - j0], F32, tag="acc", name=f"h_acc{m}_{j0}")
+            for c in range(2):
+                cols = slice(H * c + P * m, H * c + P * (m + 1))
+                nc.tensor.matmul_mx(
+                    out=acc[:],
+                    lhsT=dw_picked[:, cols].bitcast(FP8X4),
+                    lhsT_scale=ds_plane[:, cols],
+                    rhs=zw[:, j0:j1].bitcast(FP8X4),
+                    rhs_scale=zs[:, j0:j1],
+                    start=(c == 0),
+                    stop=(c == 1),
+                )
+            h = sb.tile([P, j1 - j0], F32, name=f"h{m}_{j0}")
+            nc.vector.tensor_scalar(h[:], acc[:], 0.0625, None, ALU.mult)
+            nc.scalar.activation(page[m][:].indirect(n3_sb[:, j0 // 16 : j1 // 16]), h[:], ACT.Copy)
+            if j1 == S:
+                nc.sync.dma_start(out[P * m : P * (m + 1), :], page[m][:])

@@ -66,6 +66,11 @@ def tile_picked_hdaqpolarpage_none_p_kernel(
         xs_plane = sb.tile([P, S], U8, align_bytes=64)
         nc.vector.memset(xs_plane[:].bitcast(I32), 0)
 
+        warm_in = sb.tile([P, 1], F32)
+        warm_out = sb.tile([P, 1], F32)
+        nc.vector.memset(warm_in[:], 1.0)
+        nc.scalar.activation(warm_out[:], warm_in[:], ACT.Sqrt)
+
         xs_picked = sb.tile([P, S], U8, align_bytes=64)
         nc.vector.tensor_copy(xs_picked[:], xs_table[:].indirect(offs_sb[:]))
         move_scale_rows(nc.scalar, xs_plane, xs_picked)

@@ -19,7 +19,8 @@ ACT = mybir.ActivationFunctionType
 P = 128
 PACK = 4
 QUAD = 32
-OCTET = 8
+SHIFT = 14
+MOVED = 112
 HALF = S // 2
 PIECE = 256
 
@@ -38,26 +39,30 @@ def tile_picked_hdaqpolarpage_none_p_kernel(
             nc.sync.dma_start(tile[:], src)
             return tile
 
-        def load_scale_table(queue, scales, name, tag):
-            table = sb.tile([P, scales.shape[2]], U8, name=name, tag=tag, align_bytes=64)
-            rows = scales[0].bitcast(I32)
-            queue.dma_start(table[:].bitcast(I32), rows.unsqueeze(1).to_broadcast([16, OCTET, rows.shape[1]]))
+        def load_scale_table(scales, name):
+            table = sb.tile([P, scales.shape[2]], U8, name=name, tag="scale_table", align_bytes=64)
+            for e in range(2):
+                rows = scales[0][e:16:2, :].bitcast(I32)
+                nc.sync.dma_start(table[e:P:2, :].bitcast(I32), rows.unsqueeze(1).to_broadcast([8, 8, rows.shape[1]]))
             return table
 
         def move_scale_rows(queue, plane, picked):
-            for i in range(1, 4):
-                queue.dma_start(plane[i:P:QUAD, :].bitcast(I32), picked[OCTET * i : P : QUAD, :].bitcast(I32))
+            queue.dma_start(plane[0:MOVED, :].bitcast(I32), picked[SHIFT : SHIFT + MOVED, :].bitcast(I32))
+
+        def load_w1_scales(q):
+            rows = w1_scales[0][4 * q : 4 * q + 4, :].bitcast(I32)
+            nc.sync.dma_start(w1s_raw[QUAD * q : QUAD * (q + 1), :].bitcast(I32), rows.partition_broadcast(8))
 
         offs_sb = load_list(offs, "offs_sb")
-        xw_table = sb.tile([P, T], I32, tag="word_table", align_bytes=64)
-        nc.scalar.dma_start(xw_table[:], x_words[0].rearrange("p n t -> p (n t)").bitcast(I32))
-        xs_table = load_scale_table(nc.sync, x_scales, "xs_table", "scale_table")
+        xs_table = load_scale_table(x_scales, "xs_table")
         w1w_raw = sb.tile([P, 2 * H], U8, align_bytes=64)
         nc.sync.dma_start(w1w_raw[:].bitcast(I32), w1_words[0].bitcast(I32))
         w1s_raw = sb.tile([P, H], U8, align_bytes=64)
-        for q in range(4):
-            rows = w1_scales[0][4 * q : 4 * q + 4, :].bitcast(I32)
-            nc.sync.dma_start(w1s_raw[QUAD * q : QUAD * (q + 1), :].bitcast(I32), rows.partition_broadcast(OCTET))
+        for q in range(3):
+            load_w1_scales(q)
+        xw_table = sb.tile([P, T], I32, tag="word_table", align_bytes=64)
+        nc.sync.dma_start(xw_table[:], x_words[0].rearrange("p n t -> p (n t)").bitcast(I32))
+        load_w1_scales(3)
         n1_sb = load_list(n1, "n1_sb")
         n2_sb = load_list(n2, "n2_sb")
         ka_sb = load_list(ka, "ka_sb")
@@ -65,6 +70,8 @@ def tile_picked_hdaqpolarpage_none_p_kernel(
         n3_sb = load_list(n3, "n3_sb")
         xs_plane = sb.tile([P, S], U8, align_bytes=64)
         nc.vector.memset(xs_plane[:].bitcast(I32), 0)
+        ds_plane = sb.tile([P, 2 * H], U8, align_bytes=64)
+        nc.vector.memset(ds_plane[:].bitcast(I32), 0)
 
         warm_in = sb.tile([P, 1], F32)
         warm_out = sb.tile([P, 1], F32)
@@ -74,10 +81,7 @@ def tile_picked_hdaqpolarpage_none_p_kernel(
         xs_picked = sb.tile([P, S], U8, align_bytes=64)
         nc.vector.tensor_copy(xs_picked[:], xs_table[:].indirect(offs_sb[:]))
         move_scale_rows(nc.scalar, xs_plane, xs_picked)
-        for q in range(4):
-            row = slice(QUAD * q, QUAD * q + 1)
-            nc.vector.tensor_copy(xs_plane[row, :].bitcast(I32), xs_picked[row, :].bitcast(I32))
-        ds_table = load_scale_table(nc.sync, d_scales, "ds_table", "scale_table")
+        ds_table = load_scale_table(d_scales, "ds_table")
 
         w1w = sb.tile([P, 2 * H], U8, align_bytes=64)
         nc.scalar.copy(
@@ -140,8 +144,6 @@ def tile_picked_hdaqpolarpage_none_p_kernel(
         pieces = [(H * c + s0, codes[:, s0 // 16 : (s0 + PIECE) // 16]) for c, codes in enumerate((ka_sb, kb_sb)) for s0 in range(0, H, PIECE)]
         for c0, offsets in pieces:
             nc.vector.tensor_copy(ds_picked[:, c0 : c0 + PIECE], ds_table[:].indirect(offsets))
-        ds_plane = sb.tile([P, 2 * H], U8, align_bytes=64)
-        nc.vector.tensor_copy(ds_plane[:].bitcast(I32), ds_picked[:].bitcast(I32))
         move_scale_rows(nc.sync, ds_plane, ds_picked)
         for c0, offsets in pieces:
             nc.vector.tensor_copy(dw_picked[:, c0 : c0 + PIECE], dw_table[:].bitcast(U32).indirect(offsets))

@@ -55,14 +55,13 @@ def tile_picked_hdaqpolarpage_none_p_kernel(
 
         offs_sb = load_list(offs, "offs_sb")
         xs_table = load_scale_table(x_scales, "xs_table")
-        w1w_raw = sb.tile([P, 2 * H], U8, align_bytes=64)
-        nc.sync.dma_start(w1w_raw[:].bitcast(I32), w1_words[0].bitcast(I32))
         w1s_raw = sb.tile([P, H], U8, align_bytes=64)
-        for q in range(3):
+        for q in range(4):
             load_w1_scales(q)
         xw_table = sb.tile([P, T], I32, tag="word_table", align_bytes=64)
         nc.sync.dma_start(xw_table[:], x_words[0].rearrange("p n t -> p (n t)").bitcast(I32))
-        load_w1_scales(3)
+        w1w_raw = sb.tile([P, 2 * H], U8, align_bytes=64)
+        nc.sync.dma_start(w1w_raw[:].bitcast(I32), w1_words[0].bitcast(I32))
         n1_sb = load_list(n1, "n1_sb")
         n2_sb = load_list(n2, "n2_sb")
         ka_sb = load_list(ka, "ka_sb")
@@ -84,10 +83,8 @@ def tile_picked_hdaqpolarpage_none_p_kernel(
         ds_table = load_scale_table(d_scales, "ds_table")
 
         w1w = sb.tile([P, 2 * H], U8, align_bytes=64)
-        nc.scalar.copy(
-            w1w[:].bitcast(U16).rearrange("p (t m) -> p t m", t=PACK),
-            w1w_raw[:].bitcast(U16).rearrange("p (m t) -> p t m", t=PACK),
-        )
+        for t in range(PACK):
+            nc.scalar.copy(w1w[:].bitcast(U16)[:, P * t : P * (t + 1)], w1w_raw[:].bitcast(U16)[:, t::PACK])
         w1s = sb.tile([P, H], U8, align_bytes=64)
         nc.vector.tensor_copy(
             w1s[:].rearrange("p (t m) -> p t m", t=PACK), w1s_raw[:].rearrange("p (m t) -> p t m", t=PACK)
@@ -110,8 +107,11 @@ def tile_picked_hdaqpolarpage_none_p_kernel(
                 start=True,
                 stop=True,
             )
-            y.append(sb.tile([P, S], F32, tag=f"page{t}", name=f"y{t}", align_bytes=64))
-            nc.vector.tensor_copy(y[t][:], acc[:])
+            y.append(sb.tile([P, S], F32, tag=f"y{t}", name=f"y{t}", align_bytes=64))
+            if t == 0:
+                nc.scalar.activation(y[t][:], acc[:], ACT.Copy)
+            else:
+                nc.vector.tensor_copy(y[t][:], acc[:])
 
         gs_sb = sb.tile([P, PACK], F32, tag="gs", align_bytes=64)
         nc.sync.dma_start(gs_sb[:], gs.rearrange("(p t) o -> p (t o)", t=PACK))
@@ -124,13 +124,16 @@ def tile_picked_hdaqpolarpage_none_p_kernel(
             nc.scalar.activation(pa, y[t][:].indirect(n1_sb[:]), ACT.Copy)
             nc.scalar.activation(pb, y[t][:].indirect(n2_sb[:]), ACT.Copy)
             nc.vector.scalar_tensor_tensor(rb[:, t, :], pa, -0.5, pb, ALU.mult, ALU.add)
-            squares = sb.tile([P, 2 * W], F32, name=f"squares{t}")
+            squares = sb.tile([P, 2 * W], F32, tag=f"squares{t}", name=f"squares{t}", align_bytes=64)
             nc.vector.tensor_tensor(squares[:], pair[:], pair[:], ALU.mult)
             nc.vector.scalar_tensor_tensor(radicand[:, t, :], squares[:, :W], 0.25, squares[:, W:], ALU.add, ALU.add)
 
         page = []
-        for m in range(H // P):
-            page.append(sb.tile([P, U], F32, tag=f"page{m}", name=f"page_sb{m}", align_bytes=64))
+        for m, tag in enumerate(("y0", "y1", "y3", "squares3")):
+            if m == 2:
+                dw_table2 = sb.tile([P, G], I32, tag="y2", align_bytes=64)
+                nc.sync.dma_start(dw_table2[:], d_words[0].rearrange("p n t -> p (n t)").bitcast(I32))
+            page.append(sb.tile([P, U], F32, tag=tag, name=f"page{m}", align_bytes=64))
             nc.sync.dma_start(page[m][:], mem[P * m : P * (m + 1), :])
 
         dt = [sb.tile([P, S], F32, name=f"dt{t}") for t in range(PACK)]
@@ -140,26 +143,29 @@ def tile_picked_hdaqpolarpage_none_p_kernel(
         nc.scalar.activation(ra[:], radicand[:], ACT.Sqrt)
 
         ds_picked = sb.tile([P, 2 * H], U8, align_bytes=64)
-        dw_picked = sb.tile([P, 2 * H], U32, align_bytes=64)
         pieces = [(H * c + s0, codes[:, s0 // 16 : (s0 + PIECE) // 16]) for c, codes in enumerate((ka_sb, kb_sb)) for s0 in range(0, H, PIECE)]
         for c0, offsets in pieces:
             nc.vector.tensor_copy(ds_picked[:, c0 : c0 + PIECE], ds_table[:].indirect(offsets))
         move_scale_rows(nc.sync, ds_plane, ds_picked)
-        for c0, offsets in pieces:
-            nc.vector.tensor_copy(dw_picked[:, c0 : c0 + PIECE], dw_table[:].bitcast(U32).indirect(offsets))
+        dw_first = sb.tile([P, 2, PIECE], U32, align_bytes=64)
+        for c, codes in enumerate((ka_sb, kb_sb)):
+            nc.vector.tensor_copy(dw_first[:, c, :], dw_table[:].bitcast(U32).indirect(codes[:, : PIECE // 16]))
 
-        z = [sb.tile([P, HALF, PACK], BF16, name=f"z{half}", tag=tag, align_bytes=64) for half, tag in enumerate(("scale_table", "word_table"))]
-        for t in range(PACK):
-            nc.scalar.activation(dt[t][:].indirect(n1_sb[:]), ra[:, t, :], ACT.Copy)
-            for half in range(2):
-                nc.vector.tensor_scalar(
-                    z[half][:, :, t], dt[t][:, HALF * half : HALF * (half + 1)], gs_sb[:, t : t + 1], None, ALU.mult
-                )
+        z = sb.tile([P, S, PACK], BF16, tag="word_table", align_bytes=64)
         zw = sb.tile([P, S], U32, align_bytes=64)
         zs = sb.tile([P, S], U8, align_bytes=64)
-        for half in range(2):
-            cols = slice(HALF * half, HALF * (half + 1))
-            nc.vector.quantize_mx(out=zw[:, cols].bitcast(FP8X4), scales=zs[:, cols], in_=z[half][:].rearrange("p j t -> p (j t)"))
+        for t in range(PACK):
+            nc.scalar.activation(dt[t][:].indirect(n1_sb[:]), ra[:, t, :], ACT.Copy)
+            if t < PACK - 1:
+                nc.vector.tensor_scalar(z[:, :, t], dt[t][:], gs_sb[:, t : t + 1], None, ALU.mult)
+        t = PACK - 1
+        for cols in (slice(0, HALF), slice(HALF, S)):
+            nc.vector.tensor_scalar(z[:, cols, t], dt[t][:, cols], gs_sb[:, t : t + 1], None, ALU.mult)
+            nc.vector.quantize_mx(out=zw[:, cols].bitcast(FP8X4), scales=zs[:, cols], in_=z[:, cols, :].rearrange("p j t -> p (j t)"))
+        dw_second = sb.tile([P, 2, PIECE], U32, tag="word_table", align_bytes=64)
+        for c, codes in enumerate((ka_sb, kb_sb)):
+            nc.vector.tensor_copy(dw_second[:, c, :], dw_table2[:].bitcast(U32).indirect(codes[:, PIECE // 16 :]))
+        dw_picked = [dw_first, dw_second]
 
         steps = [(0, 0, HALF), (1, 0, HALF), (0, HALF, S), (1, HALF, S), (2, 0, S), (3, 0, S)]
         for m, j0, j1 in steps:
@@ -168,7 +174,7 @@ def tile_picked_hdaqpolarpage_none_p_kernel(
                 cols = slice(H * c + P * m, H * c + P * (m + 1))
                 nc.tensor.matmul_mx(
                     out=acc[:],
-                    lhsT=dw_picked[:, cols].bitcast(FP8X4),
+                    lhsT=dw_picked[m // 2][:, c, P * (m % 2) : P * (m % 2 + 1)].bitcast(FP8X4),
                     lhsT_scale=ds_plane[:, cols],
                     rhs=zw[:, j0:j1].bitcast(FP8X4),
                     rhs_scale=zs[:, j0:j1],
@@ -176,7 +182,10 @@ def tile_picked_hdaqpolarpage_none_p_kernel(
                     stop=(c == 1),
                 )
             h = sb.tile([P, j1 - j0], F32, name=f"h{m}_{j0}")
-            nc.vector.tensor_scalar(h[:], acc[:], 0.0625, None, ALU.mult)
+            if (m, j0) == (0, 0):
+                nc.scalar.activation(h[:], acc[:], ACT.Copy, scale=0.0625)
+            else:
+                nc.vector.tensor_scalar(h[:], acc[:], 0.0625, None, ALU.mult)
             nc.scalar.activation(page[m][:].indirect(n3_sb[:, j0 // 16 : j1 // 16]), h[:], ACT.Copy)
             if j1 == S:
                 nc.sync.dma_start(out[P * m : P * (m + 1), :], page[m][:])

from contextlib import ExitStack

import concourse.mybir as mybir

K, T, S, H, W, G, U = 512, 2048, 256, 512, 128, 2048, 1024
FLOPS = 2 * K * H * S * 3

F32 = mybir.dt.float32
BF16 = mybir.dt.bfloat16
I32 = mybir.dt.int32
U32 = mybir.dt.uint32
U16 = mybir.dt.uint16
U8 = mybir.dt.uint8
FP8X4 = mybir.dt.float8_e4m3fn_x4
FP4X4 = mybir.dt.float4_e2m1fn_x4
ALU = mybir.AluOpType
ACT = mybir.ActivationFunctionType

P = 128
PACK = 4
QUAD = 32
SHIFT = 14
MOVED = 112
HALF = S // 2
PIECE = 256


def tile_picked_hdaqpolarpage_none_p_kernel(
    tc, x_words, x_scales, w1_words, w1_scales, gs, d_words, d_scales, mem, offs, n1, n2, ka, kb, n3, out
):
    nc = tc.nc
    with ExitStack() as ctx:
        lists = ctx.enter_context(tc.tile_pool(name="lists", bufs=1))
        sb = ctx.enter_context(tc.tile_pool(name="sb", bufs=1))
        psum = ctx.enter_context(tc.psum_pool(name="psum", bufs=8))

        def load_list(src, name):
            tile = lists.tile(list(src.shape), U16, name=name)
            nc.sync.dma_start(tile[:], src)
            return tile

        def load_scale_table(scales, name):
            table = sb.tile([P, scales.shape[2]], U8, name=name, tag="scale_table", align_bytes=64)
            for e in range(2):
                rows = scales[0][e:16:2, :].bitcast(I32)
                nc.sync.dma_start(table[e:P:2, :].bitcast(I32), rows.unsqueeze(1).to_broadcast([8, 8, rows.shape[1]]))
            return table

        def move_scale_rows(queue, plane, picked):
            queue.dma_start(plane[0:MOVED, :].bitcast(I32), picked[SHIFT : SHIFT + MOVED, :].bitcast(I32))

        def load_w1_scales(q):
            rows = w1_scales[0][4 * q : 4 * q + 4, :].bitcast(I32)
            nc.sync.dma_start(w1s_raw[QUAD * q : QUAD * (q + 1), :].bitcast(I32), rows.partition_broadcast(8))

        offs_sb = load_list(offs, "offs_sb")
        xs_table = load_scale_table(x_scales, "xs_table")
        w1s_raw = sb.tile([P, H], U8, align_bytes=64)
        for q in range(4):
            load_w1_scales(q)
        xw_table = sb.tile([P, T], I32, tag="word_table", align_bytes=64)
        nc.sync.dma_start(xw_table[:], x_words[0].rearrange("p n t -> p (n t)").bitcast(I32))
        w1w_raw = sb.tile([P, 2 * H], U8, align_bytes=64)
        nc.sync.dma_start(w1w_raw[:].bitcast(I32), w1_words[0].bitcast(I32))
        n1_sb = load_list(n1, "n1_sb")
        n2_sb = load_list(n2, "n2_sb")
        ka_sb = load_list(ka, "ka_sb")
        kb_sb = load_list(kb, "kb_sb")
        n3_sb = load_list(n3, "n3_sb")
        xs_plane = sb.tile([P, S], U8, align_bytes=64)
        nc.vector.memset(xs_plane[:].bitcast(I32), 0)
        ds_plane = sb.tile([P, 2 * H], U8, align_bytes=64)
        nc.vector.memset(ds_plane[:].bitcast(I32), 0)

        warm_in = sb.tile([P, 1], F32)
        warm_out = sb.tile([P, 1], F32)
        nc.vector.memset(warm_in[:], 1.0)
        nc.scalar.activation(warm_out[:], warm_in[:], ACT.Sqrt)

        xs_picked = sb.tile([P, S], U8, align_bytes=64)
        nc.vector.tensor_copy(xs_picked[:], xs_table[:].indirect(offs_sb[:]))
        move_scale_rows(nc.scalar, xs_plane, xs_picked)
        ds_table = load_scale_table(d_scales, "ds_table")

        w1w = sb.tile([P, 2 * H], U8, align_bytes=64)
        for t in range(PACK):
            nc.scalar.copy(w1w[:].bitcast(U16)[:, P * t : P * (t + 1)], w1w_raw[:].bitcast(U16)[:, t::PACK])
        w1s = sb.tile([P, H], U8, align_bytes=64)
        nc.vector.tensor_copy(
            w1s[:].rearrange("p (t m) -> p t m", t=PACK), w1s_raw[:].rearrange("p (m t) -> p t m", t=PACK)
        )
        xw_picked = sb.tile([P, S], U32, tag="gs", align_bytes=64)
        nc.vector.tensor_copy(xw_picked[:], xw_table[:].bitcast(U32).indirect(offs_sb[:]))

        dw_table = sb.tile([P, G], I32, tag="word_table", align_bytes=64)
        nc.sync.dma_start(dw_table[:], d_words[0].rearrange("p n t -> p (n t)").bitcast(I32))

        y = []
        for t in range(PACK):
            acc = psum.tile([P, S], F32, tag="acc", name=f"y_acc{t}")
            nc.tensor.matmul_mx(
                out=acc[:],
                lhsT=w1w[:, 2 * P * t : 2 * P * (t + 1)].bitcast(FP4X4),
                lhsT_scale=w1s[:, P * t : P * (t + 1)],
                rhs=xw_picked[:].bitcast(FP8X4),
                rhs_scale=xs_plane[:],
                start=True,
                stop=True,
            )
            y.append(sb.tile([P, S], F32, tag=f"y{t}", name=f"y{t}", align_bytes=64))
            if t == 0:
                nc.scalar.activation(y[t][:], acc[:], ACT.Copy)
            else:
                nc.vector.tensor_copy(y[t][:], acc[:])

        gs_sb = sb.tile([P, PACK], F32, tag="gs", align_bytes=64)
        nc.sync.dma_start(gs_sb[:], gs.rearrange("(p t) o -> p (t o)", t=PACK))

        rb = sb.tile([P, PACK, W], F32)
        radicand = sb.tile([P, PACK, W], F32)
        for t in range(PACK):
            pair = sb.tile([P, 2 * W], F32, name=f"pair{t}")
            pa, pb = pair[:, :W], pair[:, W:]
            nc.scalar.activation(pa, y[t][:].indirect(n1_sb[:]), ACT.Copy)
            nc.scalar.activation(pb, y[t][:].indirect(n2_sb[:]), ACT.Copy)
            nc.vector.scalar_tensor_tensor(rb[:, t, :], pa, -0.5, pb, ALU.mult, ALU.add)
            squares = sb.tile([P, 2 * W], F32, tag=f"squares{t}", name=f"squares{t}", align_bytes=64)
            nc.vector.tensor_tensor(squares[:], pair[:], pair[:], ALU.mult)
            nc.vector.scalar_tensor_tensor(radicand[:, t, :], squares[:, :W], 0.25, squares[:, W:], ALU.add, ALU.add)

        page = []
        for m, tag in enumerate(("y0", "y1", "y3", "squares3")):
            if m == 2:
                dw_table2 = sb.tile([P, G], I32, tag="y2", align_bytes=64)
                nc.sync.dma_start(dw_table2[:], d_words[0].rearrange("p n t -> p (n t)").bitcast(I32))
            page.append(sb.tile([P, U], F32, tag=tag, name=f"page{m}", align_bytes=64))
            nc.sync.dma_start(page[m][:], mem[P * m : P * (m + 1), :])

        dt = [sb.tile([P, S], F32, name=f"dt{t}") for t in range(PACK)]
        for t in range(PACK):
            nc.scalar.activation(dt[t][:].indirect(n2_sb[:]), rb[:, t, :], ACT.Copy)
        ra = sb.tile([P, PACK, W], F32)
        nc.scalar.activation(ra[:], radicand[:], ACT.Sqrt)

        ds_picked = sb.tile([P, 2 * H], U8, align_bytes=64)
        pieces = [(H * c + s0, codes[:, s0 // 16 : (s0 + PIECE) // 16]) for c, codes in enumerate((ka_sb, kb_sb)) for s0 in range(0, H, PIECE)]
        for c0, offsets in pieces:
            nc.vector.tensor_copy(ds_picked[:, c0 : c0 + PIECE], ds_table[:].indirect(offsets))
        move_scale_rows(nc.sync, ds_plane, ds_picked)
        dw_first = sb.tile([P, 2, PIECE], U32, align_bytes=64)
        for c, codes in enumerate((ka_sb, kb_sb)):
            nc.vector.tensor_copy(dw_first[:, c, :], dw_table[:].bitcast(U32).indirect(codes[:, : PIECE // 16]))

        z = sb.tile([P, S, PACK], BF16, tag="word_table", align_bytes=64)
        zw = sb.tile([P, S], U32, align_bytes=64)
        zs = sb.tile([P, S], U8, align_bytes=64)
        for t in range(PACK):
            nc.scalar.activation(dt[t][:].indirect(n1_sb[:]), ra[:, t, :], ACT.Copy)
            if t < PACK - 1:
                nc.vector.tensor_scalar(z[:, :, t], dt[t][:], gs_sb[:, t : t + 1], None, ALU.mult)
        t = PACK - 1
        for cols in (slice(0, HALF), slice(HALF, S)):
            nc.vector.tensor_scalar(z[:, cols, t], dt[t][:, cols], gs_sb[:, t : t + 1], None, ALU.mult)
            nc.vector.quantize_mx(out=zw[:, cols].bitcast(FP8X4), scales=zs[:, cols], in_=z[:, cols, :].rearrange("p j t -> p (j t)"))
        dw_second = sb.tile([P, 2, PIECE], U32, tag="word_table", align_bytes=64)
        for c, codes in enumerate((ka_sb, kb_sb)):
            nc.vector.tensor_copy(dw_second[:, c, :], dw_table2[:].bitcast(U32).indirect(codes[:, PIECE // 16 :]))
        dw_picked = [dw_first, dw_second]

        steps = [(0, 0, HALF), (1, 0, HALF), (0, HALF, S), (1, HALF, S), (2, 0, S), (3, 0, S)]
        for m, j0, j1 in steps:
            acc = psum.tile([P, j1 - j0], F32, tag="acc", name=f"h_acc{m}_{j0}")
            for c in range(2):
                cols = slice(H * c + P * m, H * c + P * (m + 1))
                nc.tensor.matmul_mx(
                    out=acc[:],
                    lhsT=dw_picked[m // 2][:, c, P * (m % 2) : P * (m % 2 + 1)].bitcast(FP8X4),
                    lhsT_scale=ds_plane[:, cols],
                    rhs=zw[:, j0:j1].bitcast(FP8X4),
                    rhs_scale=zs[:, j0:j1],
                    start=(c == 0),
                    stop=(c == 1),
                )
            h = sb.tile([P, j1 - j0], F32, name=f"h{m}_{j0}")
            if (m, j0) == (0, 0):
                nc.scalar.activation(h[:], acc[:], ACT.Copy, scale=0.0625)
            else:
                nc.vector.tensor_scalar(h[:], acc[:], 0.0625, None, ALU.mult)
            nc.scalar.activation(page[m][:].indirect(n3_sb[:, j0 // 16 : j1 // 16]), h[:], ACT.Copy)
            if j1 == S:
                nc.sync.dma_start(out[P * m : P * (m + 1), :], page[m][:])
